import numpy as np
import ml_dtypes


def mxq(x, axis, fmt="e4m3"):
    dtype, down = {"e4m3": (ml_dtypes.float8_e4m3fn, 7), "e5m2": (ml_dtypes.float8_e5m2, 14)}[fmt]
    v = np.moveaxis(np.asarray(x, np.float32).astype(ml_dtypes.bfloat16).astype(np.float64), axis, -1)
    blocks = v.reshape(v.shape[:-1] + (-1, 32))
    amax = np.abs(blocks).max(-1, keepdims=True)
    byte = np.maximum(np.where(amax > 0, np.frexp(amax)[1] - 1 + 127, 0) - down, 1)
    scale = np.exp2(byte - 127.0)
    codes = (blocks / scale).astype(np.float32).astype(dtype).astype(np.float64)
    return np.moveaxis((codes * scale).reshape(v.shape), -1, axis)


WIDE = False


def mx_kscale(k):
    if not WIDE:
        return np.ones(k)
    levels = np.array([10, -10, 5, -5, 0])
    if k % 512:
        return np.exp2(np.random.permutation(np.resize(levels, k // 32))).repeat(32)
    a = np.empty((k // 512, 16))
    for p in range(k // 512):
        a[p, :8] = np.random.permutation(np.resize(levels, 8))
        for g in range(8):
            far = levels[np.abs(levels - a[p, g]) >= 10]
            a[p, g + 8] = far[np.random.randint(len(far))]
    return np.exp2(a.ravel()).repeat(32)


def f64(x):
    return np.asarray(x).astype(np.float64)


def striped(idx):
    return np.tile(idx.reshape(-1, 16).T, (8, 1)).astype(np.uint16)


def unstriped(offs):
    return offs[:16].T.reshape(-1).astype(np.int64)


def striped8(idx):
    return np.concatenate([x.reshape(-1, 16).T for x in idx]).astype(np.uint16)


def runs(offs, k):
    lists = np.stack([offs[16 * r : 16 * r + 16].T.reshape(-1) for r in range(8)]).astype(np.int64)
    return lists[np.arange(k) % 512 // 64]


def pack_weight(w):
    k, n = w.shape
    w = f64(np.asarray(w, np.float32).astype(ml_dtypes.bfloat16)).reshape(k // 32, 32, n)
    amax = np.abs(w).max(1)
    byte = np.clip(np.where(amax > 0, np.frexp(amax)[1] - 1 + 127 - 7, 1), 1, 254)
    scaled = (w * np.exp2(127.0 - byte)[:, None, :]).reshape(k, n).astype(np.float32)
    words = np.ascontiguousarray(scaled.reshape(k // 512, 128, 4, n).transpose(0, 1, 3, 2)).astype(ml_dtypes.float8_e4m3fn).view(np.uint8)
    return words, np.ascontiguousarray(byte.astype(np.uint8).reshape(k // 512, 16, n))


def unpack_weight(words, scales):
    g, p, n, _ = words.shape
    vals = np.ascontiguousarray(words).view(ml_dtypes.float8_e4m3fn).astype(np.float64) * np.repeat(np.exp2(scales.astype(np.float64) - 127.0), 8, axis=1)[..., None]
    return vals.transpose(0, 1, 3, 2).reshape(g * 512, n)


def sigmoid(v):
    return 1.0 / (1.0 + np.exp(-np.maximum(v, -700.0)))

def planes(y):
    n, m = y.shape
    v = y.astype(np.float32).astype(ml_dtypes.bfloat16).astype(np.float64).reshape(n // 32, 32, m)
    top = np.abs(v).max(1)
    byte = np.clip(np.where(top > 0, np.frexp(top)[1] - 1 + 127 - 7, 1), 1, 254)
    codes = (v * np.exp2(127.0 - byte)[:, None, :]).reshape(n, m).astype(np.float32).astype(ml_dtypes.float8_e4m3fn).view(np.uint8)
    words = codes.reshape(n // 512, 128, 4, m).transpose(0, 1, 3, 2)
    return np.ascontiguousarray(words), np.ascontiguousarray(byte.astype(np.uint8).reshape(n // 512, 16, m))


K, T, S, N, H = 512, 2048, 512, 512, 512


def setup_inputs():
    n = np.random.standard_normal
    s = mx_kscale(K)[:, None]
    u = mx_kscale(H)
    packed_xT = pack_weight(n((K, T)) * s)
    packed_w1 = pack_weight(n((K, H)) / np.sqrt(K) / s)
    packed_w2 = pack_weight(n((K, H)) / np.sqrt(K) / s)
    packed_w3 = pack_weight(n((H, N)) / np.sqrt(H) / u[:, None])
    return {
        "x_words": packed_xT[0],
        "x_scales": packed_xT[1],
        "w1_words": packed_w1[0],
        "w1_scales": packed_w1[1],
        "w2_words": packed_w2[0],
        "w2_scales": packed_w2[1],
        "gn": (np.random.uniform(0.5, 1.5, (H, 1)) * u[:, None]).astype(np.float32),
        "w3_words": packed_w3[0],
        "w3_scales": packed_w3[1],
        "offs": striped(np.random.permutation(T)[:S]),
        "two": striped(np.random.permutation(T)[:S]),
        "n1": striped8(np.stack([np.random.permutation(S) for _ in range(8)])),
        "n2": striped8(np.stack([np.random.permutation(S) for _ in range(8)])),
        "n3": striped8(np.stack([np.random.permutation(S) for _ in range(8)])),
        "n4": striped8(np.stack([np.random.permutation(S) for _ in range(8)])),
    }


def reference(x_words, x_scales, w1_words, w1_scales, w2_words, w2_scales, gn, w3_words, w3_scales, offs, two, n1, n2, n3, n4):
    xq = unpack_weight(x_words, x_scales)[:, unstriped(offs)]
    y = unpack_weight(w1_words, w1_scales).T @ xq
    x_two = unpack_weight(x_words, x_scales)[:, unstriped(two)]
    d = unpack_weight(w2_words, w2_scales).T @ x_two
    z = f64(gn) * ((y + y[np.arange(H)[:, None], runs(n1, H)]) * (sigmoid(d + d[np.arange(H)[:, None], runs(n2, H)])))
    h = unpack_weight(w3_words, w3_scales).T @ mxq(z, 0, "e4m3")
    st = h * (sigmoid(h[np.arange(N)[:, None], runs(n3, N)]))
    out_0 = st - (st[np.arange(N)[:, None], runs(n4, N)])
    return (out_0,) + planes(out_0)

@@ -1,0 +1,233 @@
+from contextlib import ExitStack
+
+import concourse.mybir as mybir
+
+F32 = mybir.dt.float32
+BF16 = mybir.dt.bfloat16
+I32 = mybir.dt.int32
+U32 = mybir.dt.uint32
+U16 = mybir.dt.uint16
+U8 = mybir.dt.uint8
+FP8X4 = mybir.dt.float8_e4m3fn_x4
+ALU = mybir.AluOpType
+ACT = mybir.ActivationFunctionType
+
+P = 128
+T = 2048
+S = 512
+PACK = 4
+HALF = S // 2
+FLOPS = 3 * 2 * 512 * 512 * 512
+
+
+def tile_picked_twltriebhopg_none_po_kernel(tc, x_words, x_scales, w1_words, w1_scales, w2_words, w2_scales, gn, w3_words, w3_scales, offs, two, n1, n2, n3, n4, out_0, out_1, out_2):
+    nc = tc.nc
+    with ExitStack() as ctx:
+        lists = ctx.enter_context(tc.tile_pool(name="lists", bufs=1))
+        keep = ctx.enter_context(tc.tile_pool(name="keep", bufs=1))
+        psum = ctx.enter_context(tc.psum_pool(name="psum", bufs=1))
+
+        def sb(name, shape, dtype, tag=None):
+            return keep.tile(shape, dtype, name=name, tag=tag or name, align_bytes=64)
+
+        def load_list(name, src):
+            tile = lists.tile([P, S // 16], U16, name=name)
+            nc.sync.dma_start(tile[:], src)
+            return tile
+
+        def words_of(w):
+            return w[0].rearrange("p c r -> p (c r)").bitcast(I32)
+
+        def load_scales(tile, src, row, reps, eng=nc.sync):
+            for q in range(4):
+                rows = src[0, 4 * q : 4 * q + 4, :].bitcast(I32)
+                if reps > 1:
+                    rows = rows.unsqueeze(0).broadcast_to([reps, 4, rows.shape[1]])
+                eng.dma_start(tile[32 * q + row : 32 * q + row + 4 * reps, :].bitcast(I32), rows)
+
+        def load_words(name, words, width):
+            tile = sb(name, [P, width], I32)
+            nc.sync.dma_start(tile[:], words_of(words))
+            return tile
+
+        def deal_words(name, raw, tag=None):
+            w = sb(name, [P, S], I32, tag)
+            nc.vector.tensor_copy(w[:].rearrange("p (t c i) -> p c t i", t=PACK, i=4), raw[:].rearrange("p (c i t) -> p c t i", t=PACK, i=4))
+            return w
+
+        def deal_scales(name, raw):
+            s = sb(name, [P, S], U8)
+            nc.vector.tensor_copy(s[:].rearrange("p (t c i) -> p c t i", t=PACK, i=16), raw[:].rearrange("p (c i t) -> p c t i", t=PACK, i=16))
+            return s
+
+        ring = [sb("ring%d" % u, [P, 2 * S], F32) for u in range(2 * PACK + 1)]
+        raw13_s = sb("raw13_s", [P, S], U8)
+        nc.gpsimd.memset(raw13_s[:].bitcast(I32), 0)
+        zero = sb("zero", [P, 1], F32)
+        nc.gpsimd.memset(zero[:], 0.0)
+        nc.scalar.activation(ring[0][:, S:], zero[:].to_broadcast([P, S]), ACT.Sigmoid)
+
+        xs = sb("xs", [P, T], U8)
+        load_scales(xs, x_scales, 0, 8)
+        two_t = load_list("two_t", two)
+        offs_t = load_list("offs_t", offs)
+        xw = load_words("xw", x_words, T)
+        raw2_w = load_words("raw2_w", w2_words, S)
+        raw2_s = sb("raw2_s", [P, S], U8)
+        load_scales(raw2_s, w2_scales, 0, 8)
+        n2_t = load_list("n2_t", n2)
+        raw1_w = load_words("raw1_w", w1_words, S)
+        load_scales(raw13_s, w1_scales, 0, 1)
+        load_scales(raw13_s, w3_scales, 4, 1, nc.gpsimd)
+        gain = sb("gain", [P, PACK], F32)
+        nc.gpsimd.dma_start(gain[:], gn.rearrange("(p t) o -> p (t o)", t=PACK))
+        n1_t = load_list("n1_t", n1)
+        raw3_w = load_words("raw3_w", w3_words, S)
+        n3_t = load_list("n3_t", n3)
+        n4_t = load_list("n4_t", n4)
+
+        def pick_bytes(name, idx):
+            g = sb(name, [P, S], U8)
+            nc.vector.tensor_copy(g[:], xs[:].indirect(idx[:]))
+            return g
+
+        def pick_words(name, idx, tag=None):
+            g = sb(name, [P, S], U32, tag)
+            nc.vector.tensor_copy(g[:], xw[:].bitcast(U32).indirect(idx[:]))
+            return g
+
+        def product(out, w, t, codes, scales):
+            cols = slice(t * P, (t + 1) * P)
+            nc.tensor.matmul_mx(out=out, lhsT=w[0][:, cols].bitcast(FP8X4), lhsT_scale=w[1][w[2] :, cols], rhs=codes.bitcast(FP8X4), rhs_scale=scales, start=True, stop=True)
+
+        xs_two = pick_bytes("xs_two", two_t)
+        xs_idx = pick_bytes("xs_idx", offs_t)
+        xw_two = pick_words("xw_two", two_t)
+        w2 = (deal_words("w2_w", raw2_w), deal_scales("w2_s", raw2_s), 0)
+        d_ps = [psum.tile([P, S], F32, name="d_ps%d" % t, tag="bank%d" % t) for t in range(PACK)]
+        for t in range(PACK):
+            product(d_ps[t][:], w2, t, xw_two[:], xs_two[:])
+        xw_idx = pick_words("xw_idx", offs_t, "raw2_s")
+        w1_w = deal_words("w1_w", raw1_w)
+        s13 = deal_scales("s13", raw13_s)
+        w1 = (w1_w, s13, 0)
+        y_ps = [psum.tile([P, S], F32, name="y_ps%d" % t, tag="bank%d" % (PACK + t)) for t in range(PACK)]
+        for t in range(PACK):
+            product(y_ps[t][:], w1, t, xw_idx[:], xs_idx[:])
+
+        halves = [slice(0, HALF), slice(HALF, S)]
+        lh = [slice(0, HALF // 16), slice(HALF // 16, S // 16)]
+        ds = sb("ds", [P, PACK, S], F32, "raw13_s")
+        ys = sb("ys", [P, PACK, S], F32)
+        sg = [sb("sg%d" % h, [P, PACK, HALF], F32) for h in range(2)]
+        for t in range(PACK):
+            nc.scalar.copy(ring[t][:, :S], d_ps[t][:])
+            nc.scalar.copy(ring[t + 1][:, S:], d_ps[t][:])
+            nc.vector.tensor_tensor(ds[:, t, :], ring[t][:].indirect(n2_t[:]), ring[t + 1][:, S:], ALU.add)
+        for t in range(PACK):
+            u = PACK + t
+            nc.scalar.activation(ring[u][:, :S], y_ps[t][:], ACT.Copy, scale=gain[:, t : t + 1])
+            nc.scalar.activation(ring[u + 1][:, S:], y_ps[t][:], ACT.Copy, scale=gain[:, t : t + 1])
+            nc.vector.tensor_tensor(ys[:, t, :], ring[u][:].indirect(n1_t[:]), ring[u + 1][:, S:], ALU.add)
+        for h in range(2):
+            nc.scalar.activation(sg[h][:], ds[:, :, halves[h]], ACT.Sigmoid)
+        zb = [sb("zb%d" % h, [P, HALF * PACK], BF16) for h in range(2)]
+        zw = [sb("zw%d" % h, [P, HALF], U32) for h in range(2)]
+        zs = [sb("zs%d" % h, [P, HALF], U8) for h in range(2)]
+        h_ps = [[None] * PACK, [None] * PACK]
+        first = ring[:PACK]
+        second = [sb("second%d" % t, [P, S], F32) for t in range(PACK)]
+        nst = [sb("nst%d" % t, [P, S], F32) for t in range(PACK)]
+        nst2 = [sb("nstb%d" % t, [P, S], F32) for t in range(PACK)]
+
+        def gate(h):
+            nc.vector.tensor_tensor(
+                zb[h][:].rearrange("p (c i t) -> p c t i", t=PACK, i=4),
+                ys[:, :, halves[h]].rearrange("p t (c i) -> p c t i", i=4),
+                sg[h][:].rearrange("p t (c i) -> p c t i", i=4),
+                ALU.mult,
+            )
+
+        def third(h):
+            nc.vector.quantize_mx(out=zw[h][:].bitcast(FP8X4), scales=zs[h][:], in_=zb[h][:])
+            for t in range(PACK):
+                h_ps[h][t] = psum.tile([P, HALF], F32, name="h_ps%d%d" % (h, t), tag="bank%d" % (PACK * h + t))
+                product(h_ps[h][t][:], w3, t, zw[h][:], zs[h][:])
+
+        gate(0)
+        w3 = (deal_words("w3_w", raw3_w, "sg0"), s13, 4)
+        third(0)
+        gate(1)
+        nc.vector.tensor_copy(first[1][:, halves[0]], h_ps[0][1][:])
+        third(1)
+        nc.scalar.activation(first[0][:, halves[0]], h_ps[0][0][:], ACT.Sigmoid)
+        nc.scalar.activation(second[0][:, halves[0]], h_ps[0][0][:], ACT.Copy, scale=-1.0)
+        nc.scalar.copy(first[2][:, halves[0]], h_ps[0][2][:])
+        nc.scalar.copy(first[3][:, halves[0]], h_ps[0][3][:])
+        nc.scalar.activation(first[0][:, halves[1]], h_ps[1][0][:], ACT.Sigmoid)
+        nc.scalar.activation(second[0][:, halves[1]], h_ps[1][0][:], ACT.Copy, scale=-1.0)
+        nc.vector.tensor_copy(first[1][:, halves[1]], h_ps[1][1][:])
+        nc.vector.tensor_copy(first[2][:, halves[1]], h_ps[1][2][:])
+
+        pieces = [slice(0, 256), slice(256, 384), slice(384, 512)]
+        res = [sb("res0", [P, PACK, 256], F32)]
+
+        def diff(k, t):
+            cols = pieces[k]
+            nc.vector.tensor_tensor(res[k][:, t, :], nst[t][:].indirect(n4_t[:, cols.start // 16 : cols.stop // 16]), nst2[t][:, cols], ALU.subtract)
+
+        def look(t):
+            nc.scalar.activation(second[t][:], first[t][:].indirect(n3_t[:]), ACT.Sigmoid)
+
+        def times(t):
+            nc.vector.scalar_tensor_tensor(nst[t][:], first[t][:, :S], -1.0, second[t][:], ALU.mult, ALU.mult)
+
+        nc.vector.tensor_tensor(nst[0][:], first[0][:].indirect(n3_t[:]), second[0][:], ALU.mult)
+        look(1)
+        look(2)
+        nc.scalar.copy(first[3][:, halves[1]], h_ps[1][3][:])
+        look(3)
+        times(1)
+        nc.vector.tensor_copy(nst2[0][:], nst[0][:])
+        nc.vector.tensor_copy(nst2[1][:], nst[1][:])
+        diff(0, 0)
+        times(2)
+        nc.scalar.copy(nst2[2][:], nst[2][:])
+        diff(0, 1)
+        times(3)
+        nc.scalar.copy(nst2[3][:], nst[3][:])
+        diff(0, 2)
+        diff(0, 3)
+        res.append(sb("res1", [P, PACK, 128], F32, "second3"))
+        res.append(sb("res2", [P, PACK, 128], F32, "ring3"))
+
+        out_rows = out_0.rearrange("(p t) j -> p t j", t=PACK)
+        rb = [sb("rb%d" % k, [P, (c.stop - c.start) * PACK], BF16) for k, c in enumerate(pieces)]
+        ow = sb("ow", [P, S], I32)
+        osc = sb("osc", [P, S], U8)
+
+        def cast(k, eng):
+            nc.sync.dma_start(out_rows[:, :, pieces[k]], res[k][:])
+            dst = rb[k][:].rearrange("p (c i t) -> p c t i", t=PACK, i=4)
+            srcv = res[k][:].rearrange("p t (c i) -> p c t i", i=4)
+            eng(dst, srcv)
+
+        def quant(k):
+            nc.vector.quantize_mx(out=ow[:, pieces[k]].bitcast(FP8X4), scales=osc[:, pieces[k]], in_=rb[k][:])
+
+        cast(0, nc.scalar.copy)
+        for t in range(PACK):
+            diff(1, t)
+        cast(1, nc.scalar.copy)
+        diff(2, 0)
+        quant(0)
+        nc.sync.dma_start(words_of(out_1)[:, halves[0]], ow[:, halves[0]])
+        for t in range(1, PACK):
+            diff(2, t)
+        cast(2, nc.vector.tensor_copy)
+        quant(1)
+        quant(2)
+        nc.sync.dma_start(words_of(out_1)[:, halves[1]], ow[:, halves[1]])
+        for q in range(4):
+            eng = nc.scalar if q % 2 else nc.sync
+            eng.dma_start(out_2[0, 4 * q : 4 * q + 4, :].bitcast(I32), osc[32 * q : 32 * q + 4, :].bitcast(I32))

@@ -52,7 +52,7 @@ def tile_picked_twltriebhopg_none_po_kernel(tc, x_words, x_scales, w1_words, w1_
 
         def deal_words(name, raw, tag=None):
             w = sb(name, [P, S], I32, tag)
-            nc.vector.tensor_copy(w[:].rearrange("p (t c i) -> p c t i", t=PACK, i=4), raw[:].rearrange("p (c i t) -> p c t i", t=PACK, i=4))
+            nc.vector.tensor_copy(w[:].rearrange("p (u e c i) -> p c u i e", u=2, e=2, i=4), raw[:].rearrange("p (c i u e) -> p c u i e", u=2, e=2, i=4))
             return w
 
         def deal_scales(name, raw):
@@ -142,9 +142,9 @@ def tile_picked_twltriebhopg_none_po_kernel(tc, x_words, x_scales, w1_words, w1_
 
         def gate(h):
             nc.vector.tensor_tensor(
-                zb[h][:].rearrange("p (c i t) -> p c t i", t=PACK, i=4),
-                ys[:, :, halves[h]].rearrange("p t (c i) -> p c t i", i=4),
-                sg[h][:].rearrange("p t (c i) -> p c t i", i=4),
+                zb[h][:].rearrange("p (c i t) -> p c t i", t=PACK, i=2),
+                ys[:, :, halves[h]].rearrange("p t (c i) -> p c t i", i=2),
+                sg[h][:].rearrange("p t (c i) -> p c t i", i=2),
                 ALU.mult,
             )
 
@@ -208,8 +208,8 @@ def tile_picked_twltriebhopg_none_po_kernel(tc, x_words, x_scales, w1_words, w1_
 
         def cast(k, eng):
             nc.sync.dma_start(out_rows[:, :, pieces[k]], res[k][:])
-            dst = rb[k][:].rearrange("p (c i t) -> p c t i", t=PACK, i=4)
-            srcv = res[k][:].rearrange("p t (c i) -> p c t i", i=4)
+            dst = rb[k][:].rearrange("p (c i t) -> p c t i", t=PACK, i=2)
+            srcv = res[k][:].rearrange("p t (c i) -> p c t i", i=2)
             eng(dst, srcv)
 
         def quant(k):

@@ -78,9 +78,9 @@ def tile_picked_twltriebhopg_none_po_kernel(tc, x_words, x_scales, w1_words, w1_
         n2_t = load_list("n2_t", n2)
         raw1_w = load_words("raw1_w", w1_words, S)
         load_scales(raw13_s, w1_scales, 0, 1)
-        load_scales(raw13_s, w3_scales, 4, 1, nc.gpsimd)
+        load_scales(raw13_s, w3_scales, 4, 1)
         gain = sb("gain", [P, PACK], F32)
-        nc.gpsimd.dma_start(gain[:], gn.rearrange("(p t) o -> p (t o)", t=PACK))
+        nc.sync.dma_start(gain[:], gn.rearrange("(p t) o -> p (t o)", t=PACK))
         n1_t = load_list("n1_t", n1)
         raw3_w = load_words("raw3_w", w3_words, S)
         n3_t = load_list("n3_t", n3)
@@ -131,43 +131,52 @@ def tile_picked_twltriebhopg_none_po_kernel(tc, x_words, x_scales, w1_words, w1_
             nc.vector.tensor_tensor(ys[:, t, :], ring[u][:].indirect(n1_t[:]), ring[u + 1][:, S:], ALU.add)
         for h in range(2):
             nc.scalar.activation(sg[h][:], ds[:, :, halves[h]], ACT.Sigmoid)
-        zb = [sb("zb%d" % h, [P, HALF * PACK], BF16) for h in range(2)]
-        zw = [sb("zw%d" % h, [P, HALF], U32) for h in range(2)]
-        zs = [sb("zs%d" % h, [P, HALF], U8) for h in range(2)]
-        h_ps = [[None] * PACK, [None] * PACK]
+        zp = [slice(0, 256), slice(256, 384), slice(384, 512)]
+        zsrc = [sg[0][:], sg[1][:, :, 0:128], sg[1][:, :, 128:256]]
+        zb = [sb("zb%d" % k, [P, (c.stop - c.start) * PACK], BF16) for k, c in enumerate(zp)]
+        zw = [sb("zw%d" % k, [P, c.stop - c.start], U32) for k, c in enumerate(zp)]
+        zs = [sb("zs%d" % k, [P, c.stop - c.start], U8) for k, c in enumerate(zp)]
+        h_ps = [[None] * PACK for k in range(3)]
         first = ring[:PACK]
         second = [sb("second%d" % t, [P, S], F32) for t in range(PACK)]
         nst = [sb("nst%d" % t, [P, S], F32) for t in range(PACK)]
         nst2 = [sb("nstb%d" % t, [P, S], F32) for t in range(PACK)]
 
-        def gate(h):
+        def gate(k):
             nc.vector.tensor_tensor(
-                zb[h][:].rearrange("p (c i t) -> p c t i", t=PACK, i=2),
-                ys[:, :, halves[h]].rearrange("p t (c i) -> p c t i", i=2),
-                sg[h][:].rearrange("p t (c i) -> p c t i", i=2),
+                zb[k][:].rearrange("p (c i t) -> p c t i", t=PACK, i=2),
+                ys[:, :, zp[k]].rearrange("p t (c i) -> p c t i", i=2),
+                zsrc[k].rearrange("p t (c i) -> p c t i", i=2),
                 ALU.mult,
             )
 
-        def third(h):
-            nc.vector.quantize_mx(out=zw[h][:].bitcast(FP8X4), scales=zs[h][:], in_=zb[h][:])
+        def third(k):
+            nc.vector.quantize_mx(out=zw[k][:].bitcast(FP8X4), scales=zs[k][:], in_=zb[k][:])
             for t in range(PACK):
-                h_ps[h][t] = psum.tile([P, HALF], F32, name="h_ps%d%d" % (h, t), tag="bank%d" % (PACK * h + t))
-                product(h_ps[h][t][:], w3, t, zw[h][:], zs[h][:])
+                h_ps[k][t] = psum.tile([P, zp[k].stop - zp[k].start], F32, name="h_ps%d%d" % (k, t), tag="bank%d" % (PACK * (k % 2) + t))
+                product(h_ps[k][t][:], w3, t, zw[k][:], zs[k][:])
+
+        def lead(k):
+            nc.scalar.activation(first[0][:, zp[k]], h_ps[k][0][:], ACT.Sigmoid)
+            nc.scalar.activation(second[0][:, zp[k]], h_ps[k][0][:], ACT.Copy, scale=-1.0)
 
         gate(0)
         w3 = (deal_words("w3_w", raw3_w, "sg0"), s13, 4)
         third(0)
+        lead(0)
+        nc.scalar.copy(first[2][:, zp[0]], h_ps[0][2][:])
+        nc.scalar.copy(first[3][:, zp[0]], h_ps[0][3][:])
         gate(1)
-        nc.vector.tensor_copy(first[1][:, halves[0]], h_ps[0][1][:])
+        gate(2)
         third(1)
-        nc.scalar.activation(first[0][:, halves[0]], h_ps[0][0][:], ACT.Sigmoid)
-        nc.scalar.activation(second[0][:, halves[0]], h_ps[0][0][:], ACT.Copy, scale=-1.0)
-        nc.scalar.copy(first[2][:, halves[0]], h_ps[0][2][:])
-        nc.scalar.copy(first[3][:, halves[0]], h_ps[0][3][:])
-        nc.scalar.activation(first[0][:, halves[1]], h_ps[1][0][:], ACT.Sigmoid)
-        nc.scalar.activation(second[0][:, halves[1]], h_ps[1][0][:], ACT.Copy, scale=-1.0)
-        nc.vector.tensor_copy(first[1][:, halves[1]], h_ps[1][1][:])
-        nc.vector.tensor_copy(first[2][:, halves[1]], h_ps[1][2][:])
+        nc.vector.tensor_copy(first[1][:, zp[0]], h_ps[0][1][:])
+        third(2)
+        lead(1)
+        lead(2)
+        for k in (1, 2):
+            nc.vector.tensor_copy(first[1][:, zp[k]], h_ps[k][1][:])
+        for k in (1, 2):
+            nc.vector.tensor_copy(first[2][:, zp[k]], h_ps[k][2][:])
 
         pieces = [slice(0, 256), slice(256, 384), slice(384, 512)]
         res = [sb("res0", [P, PACK, 256], F32)]
@@ -185,7 +194,8 @@ def tile_picked_twltriebhopg_none_po_kernel(tc, x_words, x_scales, w1_words, w1_
         nc.vector.tensor_tensor(nst[0][:], first[0][:].indirect(n3_t[:]), second[0][:], ALU.mult)
         look(1)
         look(2)
-        nc.scalar.copy(first[3][:, halves[1]], h_ps[1][3][:])
+        for k in (1, 2):
+            nc.scalar.copy(first[3][:, zp[k]], h_ps[k][3][:])
         look(3)
         times(1)
         nc.vector.tensor_copy(nst2[0][:], nst[0][:])

@@ -15,8 +15,11 @@ ACT = mybir.ActivationFunctionType
 P = 128
 T = 2048
 S = 512
-PACK = 4
-HALF = S // 2
+SLOTS = 4
+QUADS = 4
+W3_ROW = 4
+HALVES = (slice(0, S // 2), slice(S // 2, S))
+PIECES = (slice(0, 256), slice(256, 384), slice(384, 512))
 FLOPS = 3 * 2 * 512 * 512 * 512
 
 
@@ -27,217 +30,222 @@ def tile_picked_twltriebhopg_none_po_kernel(tc, x_words, x_scales, w1_words, w1_
         keep = ctx.enter_context(tc.tile_pool(name="keep", bufs=1))
         psum = ctx.enter_context(tc.psum_pool(name="psum", bufs=1))
 
-        def sb(name, shape, dtype, tag=None):
-            return keep.tile(shape, dtype, name=name, tag=tag or name, align_bytes=64)
+        def sbuf(name, shape, dtype, reuse=None):
+            return keep.tile(shape, dtype, name=name, tag=reuse or name, align_bytes=64)
+
+        def width(cols):
+            return cols.stop - cols.start
+
+        def words_of(packed):
+            return packed[0].rearrange("p c r -> p (c r)").bitcast(I32)
 
         def load_list(name, src):
             tile = lists.tile([P, S // 16], U16, name=name)
             nc.sync.dma_start(tile[:], src)
             return tile
 
-        def words_of(w):
-            return w[0].rearrange("p c r -> p (c r)").bitcast(I32)
-
-        def load_scales(tile, src, row, reps, eng=nc.sync):
-            for q in range(4):
-                rows = src[0, 4 * q : 4 * q + 4, :].bitcast(I32)
-                if reps > 1:
-                    rows = rows.unsqueeze(0).broadcast_to([reps, 4, rows.shape[1]])
-                eng.dma_start(tile[32 * q + row : 32 * q + row + 4 * reps, :].bitcast(I32), rows)
-
-        def load_words(name, words, width):
-            tile = sb(name, [P, width], I32)
-            nc.sync.dma_start(tile[:], words_of(words))
+        def load_words(name, packed, columns):
+            tile = sbuf(name, [P, columns], I32)
+            nc.sync.dma_start(tile[:], words_of(packed))
             return tile
 
-        def deal_words(name, raw, tag=None):
-            w = sb(name, [P, S], I32, tag)
-            nc.vector.tensor_copy(w[:].rearrange("p (u e c i) -> p c u i e", u=2, e=2, i=4), raw[:].rearrange("p (c i u e) -> p c u i e", u=2, e=2, i=4))
-            return w
+        def load_scale_rows(tile, scales, first_row):
+            for q in range(QUADS):
+                nc.sync.dma_start(tile[32 * q + first_row : 32 * q + first_row + 4, :].bitcast(I32), scales[0, 4 * q : 4 * q + 4, :].bitcast(I32))
+
+        def load_scale_rows_repeated(tile, scales):
+            for q in range(QUADS):
+                rows = scales[0, 4 * q : 4 * q + 4, :].bitcast(I32)
+                nc.sync.dma_start(tile[32 * q : 32 * q + 32, :].bitcast(I32), rows.unsqueeze(0).broadcast_to([8, 4, rows.shape[1]]))
+
+        def deal_words(name, raw, reuse=None):
+            dealt = sbuf(name, [P, S], I32, reuse)
+            nc.vector.tensor_copy(dealt[:].rearrange("p (u e c i) -> p c u i e", u=2, e=2, i=4), raw[:].rearrange("p (c i u e) -> p c u i e", u=2, e=2, i=4))
+            return dealt
 
         def deal_scales(name, raw):
-            s = sb(name, [P, S], U8)
-            nc.vector.tensor_copy(s[:].rearrange("p (t c i) -> p c t i", t=PACK, i=16), raw[:].rearrange("p (c i t) -> p c t i", t=PACK, i=16))
-            return s
+            dealt = sbuf(name, [P, S], U8)
+            nc.vector.tensor_copy(dealt[:].rearrange("p (t c i) -> p c t i", t=SLOTS, i=16), raw[:].rearrange("p (c i t) -> p c t i", t=SLOTS, i=16))
+            return dealt
 
-        ring = [sb("ring%d" % u, [P, 2 * S], F32) for u in range(2 * PACK + 1)]
-        raw13_s = sb("raw13_s", [P, S], U8)
+        def by_words(tile):
+            return tile[:].rearrange("p (c i t) -> p c t i", t=SLOTS, i=2)
+
+        def by_slots(view):
+            return view.rearrange("p t (c i) -> p c t i", i=2)
+
+        chain = [sbuf("chain%d" % u, [P, 2 * S], F32) for u in range(2 * SLOTS + 1)]
+        raw13_s = sbuf("raw13_s", [P, S], U8)
         nc.gpsimd.memset(raw13_s[:].bitcast(I32), 0)
-        zero = sb("zero", [P, 1], F32)
+        zero = sbuf("zero", [P, 1], F32)
         nc.gpsimd.memset(zero[:], 0.0)
-        nc.scalar.activation(ring[0][:, S:], zero[:].to_broadcast([P, S]), ACT.Sigmoid)
+        nc.scalar.activation(chain[0][:, S:], zero[:].to_broadcast([P, S]), ACT.Sigmoid)
 
-        xs = sb("xs", [P, T], U8)
-        load_scales(xs, x_scales, 0, 8)
+        x_s = sbuf("x_s", [P, T], U8)
+        load_scale_rows_repeated(x_s, x_scales)
         two_t = load_list("two_t", two)
         offs_t = load_list("offs_t", offs)
-        xw = load_words("xw", x_words, T)
+        x_w = load_words("x_w", x_words, T)
         raw2_w = load_words("raw2_w", w2_words, S)
-        raw2_s = sb("raw2_s", [P, S], U8)
-        load_scales(raw2_s, w2_scales, 0, 8)
-        n2_t = load_list("n2_t", n2)
+        raw2_s = sbuf("raw2_s", [P, S], U8)
+        nc.gpsimd.memset(raw2_s[:].bitcast(I32), 0)
+        load_scale_rows(raw2_s, w2_scales, 0)
+        load_scale_rows(raw13_s, w1_scales, 0)
+        load_scale_rows(raw13_s, w3_scales, W3_ROW)
         raw1_w = load_words("raw1_w", w1_words, S)
-        load_scales(raw13_s, w1_scales, 0, 1)
-        load_scales(raw13_s, w3_scales, 4, 1)
-        gain = sb("gain", [P, PACK], F32)
-        nc.sync.dma_start(gain[:], gn.rearrange("(p t) o -> p (t o)", t=PACK))
+        n2_t = load_list("n2_t", n2)
+        gain = sbuf("gain", [P, SLOTS], F32)
+        nc.sync.dma_start(gain[:], gn.rearrange("(p t) o -> p (t o)", t=SLOTS))
         n1_t = load_list("n1_t", n1)
         raw3_w = load_words("raw3_w", w3_words, S)
         n3_t = load_list("n3_t", n3)
         n4_t = load_list("n4_t", n4)
 
-        def pick_bytes(name, idx):
-            g = sb(name, [P, S], U8)
-            nc.vector.tensor_copy(g[:], xs[:].indirect(idx[:]))
-            return g
+        def pick_bytes(name, entries):
+            picked = sbuf(name, [P, S], U8)
+            nc.vector.tensor_copy(picked[:], x_s[:].indirect(entries[:]))
+            return picked
 
-        def pick_words(name, idx, tag=None):
-            g = sb(name, [P, S], U32, tag)
-            nc.vector.tensor_copy(g[:], xw[:].bitcast(U32).indirect(idx[:]))
-            return g
+        def pick_words(name, entries, reuse=None):
+            picked = sbuf(name, [P, S], U32, reuse)
+            nc.vector.tensor_copy(picked[:], x_w[:].bitcast(U32).indirect(entries[:]))
+            return picked
 
-        def product(out, w, t, codes, scales):
+        def product(out, weight, t, codes, scales):
+            words, scale_tile, first_row = weight
             cols = slice(t * P, (t + 1) * P)
-            nc.tensor.matmul_mx(out=out, lhsT=w[0][:, cols].bitcast(FP8X4), lhsT_scale=w[1][w[2] :, cols], rhs=codes.bitcast(FP8X4), rhs_scale=scales, start=True, stop=True)
+            nc.tensor.matmul_mx(out=out, lhsT=words[:, cols].bitcast(FP8X4), lhsT_scale=scale_tile[first_row:, cols], rhs=codes.bitcast(FP8X4), rhs_scale=scales, start=True, stop=True)
 
-        xs_two = pick_bytes("xs_two", two_t)
-        xs_idx = pick_bytes("xs_idx", offs_t)
-        xw_two = pick_words("xw_two", two_t)
+        two_s = pick_bytes("two_s", two_t)
+        idx_s = pick_bytes("idx_s", offs_t)
+        two_w = pick_words("two_w", two_t)
         w2 = (deal_words("w2_w", raw2_w), deal_scales("w2_s", raw2_s), 0)
-        d_ps = [psum.tile([P, S], F32, name="d_ps%d" % t, tag="bank%d" % t) for t in range(PACK)]
-        for t in range(PACK):
-            product(d_ps[t][:], w2, t, xw_two[:], xs_two[:])
-        xw_idx = pick_words("xw_idx", offs_t, "raw2_s")
-        w1_w = deal_words("w1_w", raw1_w)
-        s13 = deal_scales("s13", raw13_s)
-        w1 = (w1_w, s13, 0)
-        y_ps = [psum.tile([P, S], F32, name="y_ps%d" % t, tag="bank%d" % (PACK + t)) for t in range(PACK)]
-        for t in range(PACK):
-            product(y_ps[t][:], w1, t, xw_idx[:], xs_idx[:])
+        d_ps = [psum.tile([P, S], F32, name="d_ps%d" % t, tag="bank%d" % t) for t in range(SLOTS)]
+        for t in range(SLOTS):
+            product(d_ps[t][:], w2, t, two_w[:], two_s[:])
+        idx_w = pick_words("idx_w", offs_t, "raw2_s")
+        w13_s = deal_scales("w13_s", raw13_s)
+        w1 = (deal_words("w1_w", raw1_w), w13_s, 0)
+        y_ps = [psum.tile([P, S], F32, name="y_ps%d" % t, tag="bank%d" % (SLOTS + t)) for t in range(SLOTS)]
+        for t in range(SLOTS):
+            product(y_ps[t][:], w1, t, idx_w[:], idx_s[:])
 
-        halves = [slice(0, HALF), slice(HALF, S)]
-        lh = [slice(0, HALF // 16), slice(HALF // 16, S // 16)]
-        ds = sb("ds", [P, PACK, S], F32, "raw13_s")
-        ys = sb("ys", [P, PACK, S], F32)
-        sg = [sb("sg%d" % h, [P, PACK, HALF], F32) for h in range(2)]
-        for t in range(PACK):
-            nc.scalar.copy(ring[t][:, :S], d_ps[t][:])
-            nc.scalar.copy(ring[t + 1][:, S:], d_ps[t][:])
-            nc.vector.tensor_tensor(ds[:, t, :], ring[t][:].indirect(n2_t[:]), ring[t + 1][:, S:], ALU.add)
-        for t in range(PACK):
-            u = PACK + t
-            nc.scalar.activation(ring[u][:, :S], y_ps[t][:], ACT.Copy, scale=gain[:, t : t + 1])
-            nc.scalar.activation(ring[u + 1][:, S:], y_ps[t][:], ACT.Copy, scale=gain[:, t : t + 1])
-            nc.vector.tensor_tensor(ys[:, t, :], ring[u][:].indirect(n1_t[:]), ring[u + 1][:, S:], ALU.add)
-        for h in range(2):
-            nc.scalar.activation(sg[h][:], ds[:, :, halves[h]], ACT.Sigmoid)
-        zp = [slice(0, 256), slice(256, 384), slice(384, 512)]
-        zsrc = [sg[0][:], sg[1][:, :, 0:128], sg[1][:, :, 128:256]]
-        zb = [sb("zb%d" % k, [P, (c.stop - c.start) * PACK], BF16) for k, c in enumerate(zp)]
-        zw = [sb("zw%d" % k, [P, c.stop - c.start], U32) for k, c in enumerate(zp)]
-        zs = [sb("zs%d" % k, [P, c.stop - c.start], U8) for k, c in enumerate(zp)]
-        h_ps = [[None] * PACK for k in range(3)]
-        first = ring[:PACK]
-        second = [sb("second%d" % t, [P, S], F32) for t in range(PACK)]
-        nst = [sb("nst%d" % t, [P, S], F32) for t in range(PACK)]
-        nst2 = [sb("nstb%d" % t, [P, S], F32) for t in range(PACK)]
+        d_sum = sbuf("d_sum", [P, SLOTS, S], F32, "raw1_w")
+        y_sum = sbuf("y_sum", [P, SLOTS, S], F32)
+        d_sig = [sbuf("d_sig%d" % half, [P, SLOTS, S // 2], F32) for half in range(2)]
+        for t in range(SLOTS):
+            nc.scalar.copy(chain[t][:, :S], d_ps[t][:])
+            nc.scalar.copy(chain[t + 1][:, S:], d_ps[t][:])
+            nc.vector.tensor_tensor(d_sum[:, t, :], chain[t][:].indirect(n2_t[:]), chain[t + 1][:, S:], ALU.add)
+        for t in range(SLOTS):
+            u = SLOTS + t
+            nc.scalar.activation(chain[u][:, :S], y_ps[t][:], ACT.Copy, scale=gain[:, t : t + 1])
+            nc.scalar.activation(chain[u + 1][:, S:], y_ps[t][:], ACT.Copy, scale=gain[:, t : t + 1])
+            nc.vector.tensor_tensor(y_sum[:, t, :], chain[u][:].indirect(n1_t[:]), chain[u + 1][:, S:], ALU.add)
+        for half in range(2):
+            nc.scalar.activation(d_sig[half][:], d_sum[:, :, HALVES[half]], ACT.Sigmoid)
 
-        def gate(k):
-            nc.vector.tensor_tensor(
-                zb[k][:].rearrange("p (c i t) -> p c t i", t=PACK, i=2),
-                ys[:, :, zp[k]].rearrange("p t (c i) -> p c t i", i=2),
-                zsrc[k].rearrange("p t (c i) -> p c t i", i=2),
-                ALU.mult,
-            )
+        piece_sig = (d_sig[0][:], d_sig[1][:, :, : width(PIECES[1])], d_sig[1][:, :, width(PIECES[1]) :])
+        z_bf = [sbuf("z_bf%d" % k, [P, width(cols) * SLOTS], BF16) for k, cols in enumerate(PIECES)]
+        z_w = [sbuf("z_w%d" % k, [P, width(cols)], U32) for k, cols in enumerate(PIECES)]
+        z_s = [sbuf("z_s%d" % k, [P, width(cols)], U8) for k, cols in enumerate(PIECES)]
+        h_ps = [[None] * SLOTS for cols in PIECES]
+        window = chain[:SLOTS]
+        partner = [sbuf("partner%d" % t, [P, S], F32) for t in range(SLOTS)]
+        neg_st = [sbuf("neg_st%d" % t, [P, S], F32) for t in range(SLOTS)]
+        neg_st_plain = [sbuf("neg_st_plain%d" % t, [P, S], F32) for t in range(SLOTS)]
 
-        def third(k):
-            nc.vector.quantize_mx(out=zw[k][:].bitcast(FP8X4), scales=zs[k][:], in_=zb[k][:])
-            for t in range(PACK):
-                h_ps[k][t] = psum.tile([P, zp[k].stop - zp[k].start], F32, name="h_ps%d%d" % (k, t), tag="bank%d" % (PACK * (k % 2) + t))
-                product(h_ps[k][t][:], w3, t, zw[k][:], zs[k][:])
+        def make_z(k):
+            nc.vector.tensor_tensor(by_words(z_bf[k]), by_slots(y_sum[:, :, PIECES[k]]), by_slots(piece_sig[k]), ALU.mult)
 
-        def lead(k):
-            nc.scalar.activation(first[0][:, zp[k]], h_ps[k][0][:], ACT.Sigmoid)
-            nc.scalar.activation(second[0][:, zp[k]], h_ps[k][0][:], ACT.Copy, scale=-1.0)
+        def make_h(k):
+            nc.vector.quantize_mx(out=z_w[k][:].bitcast(FP8X4), scales=z_s[k][:], in_=z_bf[k][:])
+            for t in range(SLOTS):
+                h_ps[k][t] = psum.tile([P, width(PIECES[k])], F32, name="h_ps%d%d" % (k, t), tag="bank%d" % (SLOTS * (k % 2) + t))
+                product(h_ps[k][t][:], w3, t, z_w[k][:], z_s[k][:])
 
-        gate(0)
-        w3 = (deal_words("w3_w", raw3_w, "sg0"), s13, 4)
-        third(0)
-        lead(0)
-        nc.scalar.copy(first[2][:, zp[0]], h_ps[0][2][:])
-        nc.scalar.copy(first[3][:, zp[0]], h_ps[0][3][:])
-        gate(1)
-        gate(2)
-        third(1)
-        nc.vector.tensor_copy(first[1][:, zp[0]], h_ps[0][1][:])
-        third(2)
-        lead(1)
-        lead(2)
+        def leave_slot_0(k):
+            nc.scalar.activation(window[0][:, PIECES[k]], h_ps[k][0][:], ACT.Sigmoid)
+            nc.scalar.activation(partner[0][:, PIECES[k]], h_ps[k][0][:], ACT.Copy, scale=-1.0)
+
+        def leave(copy, k, t):
+            copy(window[t][:, PIECES[k]], h_ps[k][t][:])
+
+        make_z(0)
+        w3 = (deal_words("w3_w", raw3_w, "d_sig0"), w13_s, W3_ROW)
+        make_h(0)
+        leave_slot_0(0)
+        leave(nc.scalar.copy, 0, 2)
+        leave(nc.scalar.copy, 0, 3)
+        make_z(1)
+        make_z(2)
+        make_h(1)
+        leave(nc.vector.tensor_copy, 0, 1)
+        make_h(2)
+        leave_slot_0(1)
+        leave_slot_0(2)
+        for t in (1, 2):
+            for k in (1, 2):
+                leave(nc.vector.tensor_copy, k, t)
+
+        result = [sbuf("result0", [P, SLOTS, width(PIECES[0])], F32)]
+
+        def look_up_sigmoid(t):
+            nc.scalar.activation(partner[t][:], window[t][:].indirect(n3_t[:]), ACT.Sigmoid)
+
+        def make_neg_st(t):
+            nc.vector.scalar_tensor_tensor(neg_st[t][:], window[t][:, :S], -1.0, partner[t][:], ALU.mult, ALU.mult)
+
+        def make_result(k, t):
+            cols = PIECES[k]
+            nc.vector.tensor_tensor(result[k][:, t, :], neg_st[t][:].indirect(n4_t[:, cols.start // 16 : cols.stop // 16]), neg_st_plain[t][:, cols], ALU.subtract)
+
+        nc.vector.tensor_tensor(neg_st[0][:], window[0][:].indirect(n3_t[:]), partner[0][:], ALU.mult)
+        look_up_sigmoid(1)
+        look_up_sigmoid(2)
         for k in (1, 2):
-            nc.vector.tensor_copy(first[1][:, zp[k]], h_ps[k][1][:])
-        for k in (1, 2):
-            nc.vector.tensor_copy(first[2][:, zp[k]], h_ps[k][2][:])
+            leave(nc.scalar.copy, k, 3)
+        look_up_sigmoid(3)
+        make_neg_st(1)
+        nc.vector.tensor_copy(neg_st_plain[0][:], neg_st[0][:])
+        nc.vector.tensor_copy(neg_st_plain[1][:], neg_st[1][:])
+        for t in (2, 3):
+            make_result(0, t - 2)
+            make_neg_st(t)
+            nc.scalar.copy(neg_st_plain[t][:], neg_st[t][:])
+        make_result(0, 2)
+        make_result(0, 3)
+        result.append(sbuf("result1", [P, SLOTS, width(PIECES[1])], F32, "partner3"))
+        result.append(sbuf("result2", [P, SLOTS, width(PIECES[2])], F32, "chain3"))
 
-        pieces = [slice(0, 256), slice(256, 384), slice(384, 512)]
-        res = [sb("res0", [P, PACK, 256], F32)]
+        out_rows = out_0.rearrange("(p t) j -> p t j", t=SLOTS)
+        out_bf = [sbuf("out_bf%d" % k, [P, width(cols) * SLOTS], BF16) for k, cols in enumerate(PIECES)]
+        out_w = sbuf("out_w", [P, S], I32)
+        out_s = sbuf("out_s", [P, S], U8)
 
-        def diff(k, t):
-            cols = pieces[k]
-            nc.vector.tensor_tensor(res[k][:, t, :], nst[t][:].indirect(n4_t[:, cols.start // 16 : cols.stop // 16]), nst2[t][:, cols], ALU.subtract)
+        def store_and_round(k, copy):
+            nc.sync.dma_start(out_rows[:, :, PIECES[k]], result[k][:])
+            copy(by_words(out_bf[k]), by_slots(result[k][:]))
 
-        def look(t):
-            nc.scalar.activation(second[t][:], first[t][:].indirect(n3_t[:]), ACT.Sigmoid)
+        def quantise_out(k):
+            nc.vector.quantize_mx(out=out_w[:, PIECES[k]].bitcast(FP8X4), scales=out_s[:, PIECES[k]], in_=out_bf[k][:])
 
-        def times(t):
-            nc.vector.scalar_tensor_tensor(nst[t][:], first[t][:, :S], -1.0, second[t][:], ALU.mult, ALU.mult)
+        def store_words(half):
+            nc.sync.dma_start(words_of(out_1)[:, HALVES[half]], out_w[:, HALVES[half]])
 
-        nc.vector.tensor_tensor(nst[0][:], first[0][:].indirect(n3_t[:]), second[0][:], ALU.mult)
-        look(1)
-        look(2)
-        for k in (1, 2):
-            nc.scalar.copy(first[3][:, zp[k]], h_ps[k][3][:])
-        look(3)
-        times(1)
-        nc.vector.tensor_copy(nst2[0][:], nst[0][:])
-        nc.vector.tensor_copy(nst2[1][:], nst[1][:])
-        diff(0, 0)
-        times(2)
-        nc.scalar.copy(nst2[2][:], nst[2][:])
-        diff(0, 1)
-        times(3)
-        nc.scalar.copy(nst2[3][:], nst[3][:])
-        diff(0, 2)
-        diff(0, 3)
-        res.append(sb("res1", [P, PACK, 128], F32, "second3"))
-        res.append(sb("res2", [P, PACK, 128], F32, "ring3"))
-
-        out_rows = out_0.rearrange("(p t) j -> p t j", t=PACK)
-        rb = [sb("rb%d" % k, [P, (c.stop - c.start) * PACK], BF16) for k, c in enumerate(pieces)]
-        ow = sb("ow", [P, S], I32)
-        osc = sb("osc", [P, S], U8)
-
-        def cast(k, eng):
-            nc.sync.dma_start(out_rows[:, :, pieces[k]], res[k][:])
-            dst = rb[k][:].rearrange("p (c i t) -> p c t i", t=PACK, i=2)
-            srcv = res[k][:].rearrange("p t (c i) -> p c t i", i=2)
-            eng(dst, srcv)
-
-        def quant(k):
-            nc.vector.quantize_mx(out=ow[:, pieces[k]].bitcast(FP8X4), scales=osc[:, pieces[k]], in_=rb[k][:])
-
-        cast(0, nc.scalar.copy)
-        for t in range(PACK):
-            diff(1, t)
-        cast(1, nc.scalar.copy)
-        diff(2, 0)
-        quant(0)
-        nc.sync.dma_start(words_of(out_1)[:, halves[0]], ow[:, halves[0]])
-        for t in range(1, PACK):
-            diff(2, t)
-        cast(2, nc.vector.tensor_copy)
-        quant(1)
-        quant(2)
-        nc.sync.dma_start(words_of(out_1)[:, halves[1]], ow[:, halves[1]])
-        for q in range(4):
-            eng = nc.scalar if q % 2 else nc.sync
-            eng.dma_start(out_2[0, 4 * q : 4 * q + 4, :].bitcast(I32), osc[32 * q : 32 * q + 4, :].bitcast(I32))
+        store_and_round(0, nc.scalar.copy)
+        for t in range(SLOTS):
+            make_result(1, t)
+        store_and_round(1, nc.scalar.copy)
+        make_result(2, 0)
+        quantise_out(0)
+        store_words(0)
+        for t in range(1, SLOTS):
+            make_result(2, t)
+        store_and_round(2, nc.vector.tensor_copy)
+        quantise_out(1)
+        quantise_out(2)
+        store_words(1)
+        for q in range(QUADS):
+            queue = nc.scalar if q % 2 else nc.sync
+            queue.dma_start(out_2[0, 4 * q : 4 * q + 4, :].bitcast(I32), out_s[32 * q : 32 * q + 4, :].bitcast(I32))

from contextlib import ExitStack

import concourse.mybir as mybir

F32 = mybir.dt.float32
BF16 = mybir.dt.bfloat16
I32 = mybir.dt.int32
U32 = mybir.dt.uint32
U16 = mybir.dt.uint16
U8 = mybir.dt.uint8
FP8X4 = mybir.dt.float8_e4m3fn_x4
ALU = mybir.AluOpType
ACT = mybir.ActivationFunctionType

P = 128
T = 2048
S = 512
SLOTS = 4
QUADS = 4
W3_ROW = 4
HALVES = (slice(0, S // 2), slice(S // 2, S))
PIECES = (slice(0, 256), slice(256, 384), slice(384, 512))
FLOPS = 3 * 2 * 512 * 512 * 512


def tile_picked_twltriebhopg_none_po_kernel(tc, x_words, x_scales, w1_words, w1_scales, w2_words, w2_scales, gn, w3_words, w3_scales, offs, two, n1, n2, n3, n4, out_0, out_1, out_2):
    nc = tc.nc
    with ExitStack() as ctx:
        lists = ctx.enter_context(tc.tile_pool(name="lists", bufs=1))
        keep = ctx.enter_context(tc.tile_pool(name="keep", bufs=1))
        psum = ctx.enter_context(tc.psum_pool(name="psum", bufs=1))

        def sbuf(name, shape, dtype, reuse=None):
            return keep.tile(shape, dtype, name=name, tag=reuse or name, align_bytes=64)

        def width(cols):
            return cols.stop - cols.start

        def words_of(packed):
            return packed[0].rearrange("p c r -> p (c r)").bitcast(I32)

        def load_list(name, src):
            tile = lists.tile([P, S // 16], U16, name=name)
            nc.sync.dma_start(tile[:], src)
            return tile

        def load_words(name, packed, columns):
            tile = sbuf(name, [P, columns], I32)
            nc.sync.dma_start(tile[:], words_of(packed))
            return tile

        def load_scale_rows(tile, scales, first_row):
            for q in range(QUADS):
                nc.sync.dma_start(tile[32 * q + first_row : 32 * q + first_row + 4, :].bitcast(I32), scales[0, 4 * q : 4 * q + 4, :].bitcast(I32))

        def load_scale_rows_repeated(tile, scales):
            for q in range(QUADS):
                rows = scales[0, 4 * q : 4 * q + 4, :].bitcast(I32)
                nc.sync.dma_start(tile[32 * q : 32 * q + 32, :].bitcast(I32), rows.unsqueeze(0).broadcast_to([8, 4, rows.shape[1]]))

        def deal_words(name, raw, reuse=None):
            dealt = sbuf(name, [P, S], I32, reuse)
            nc.vector.tensor_copy(dealt[:].rearrange("p (u e c i) -> p c u i e", u=2, e=2, i=4), raw[:].rearrange("p (c i u e) -> p c u i e", u=2, e=2, i=4))
            return dealt

        def deal_scales(name, raw):
            dealt = sbuf(name, [P, S], U8)
            nc.vector.tensor_copy(dealt[:].rearrange("p (t c i) -> p c t i", t=SLOTS, i=16), raw[:].rearrange("p (c i t) -> p c t i", t=SLOTS, i=16))
            return dealt

        def by_words(tile):
            return tile[:].rearrange("p (c i t) -> p c t i", t=SLOTS, i=2)

        def by_slots(view):
            return view.rearrange("p t (c i) -> p c t i", i=2)

        chain = [sbuf("chain%d" % u, [P, 2 * S], F32) for u in range(2 * SLOTS + 1)]
        raw13_s = sbuf("raw13_s", [P, S], U8)
        nc.gpsimd.memset(raw13_s[:].bitcast(I32), 0)
        zero = sbuf("zero", [P, 1], F32)
        nc.gpsimd.memset(zero[:], 0.0)
        nc.scalar.activation(chain[0][:, S:], zero[:].to_broadcast([P, S]), ACT.Sigmoid)

        x_s = sbuf("x_s", [P, T], U8)
        load_scale_rows_repeated(x_s, x_scales)
        two_t = load_list("two_t", two)
        offs_t = load_list("offs_t", offs)
        x_w = load_words("x_w", x_words, T)
        raw2_w = load_words("raw2_w", w2_words, S)
        raw2_s = sbuf("raw2_s", [P, S], U8)
        nc.gpsimd.memset(raw2_s[:].bitcast(I32), 0)
        load_scale_rows(raw2_s, w2_scales, 0)
        load_scale_rows(raw13_s, w1_scales, 0)
        load_scale_rows(raw13_s, w3_scales, W3_ROW)
        raw1_w = load_words("raw1_w", w1_words, S)
        n2_t = load_list("n2_t", n2)
        gain = sbuf("gain", [P, SLOTS], F32)
        nc.sync.dma_start(gain[:], gn.rearrange("(p t) o -> p (t o)", t=SLOTS))
        n1_t = load_list("n1_t", n1)
        raw3_w = load_words("raw3_w", w3_words, S)
        n3_t = load_list("n3_t", n3)
        n4_t = load_list("n4_t", n4)

        def pick_bytes(name, entries):
            picked = sbuf(name, [P, S], U8)
            nc.vector.tensor_copy(picked[:], x_s[:].indirect(entries[:]))
            return picked

        def pick_words(name, entries, reuse=None):
            picked = sbuf(name, [P, S], U32, reuse)
            nc.vector.tensor_copy(picked[:], x_w[:].bitcast(U32).indirect(entries[:]))
            return picked

        def product(out, weight, t, codes, scales):
            words, scale_tile, first_row = weight
            cols = slice(t * P, (t + 1) * P)
            nc.tensor.matmul_mx(out=out, lhsT=words[:, cols].bitcast(FP8X4), lhsT_scale=scale_tile[first_row:, cols], rhs=codes.bitcast(FP8X4), rhs_scale=scales, start=True, stop=True)

        two_s = pick_bytes("two_s", two_t)
        idx_s = pick_bytes("idx_s", offs_t)
        two_w = pick_words("two_w", two_t)
        w2 = (deal_words("w2_w", raw2_w), deal_scales("w2_s", raw2_s), 0)
        d_ps = [psum.tile([P, S], F32, name="d_ps%d" % t, tag="bank%d" % t) for t in range(SLOTS)]
        for t in range(SLOTS):
            product(d_ps[t][:], w2, t, two_w[:], two_s[:])
        idx_w = pick_words("idx_w", offs_t, "raw2_s")
        w13_s = deal_scales("w13_s", raw13_s)
        w1 = (deal_words("w1_w", raw1_w), w13_s, 0)
        y_ps = [psum.tile([P, S], F32, name="y_ps%d" % t, tag="bank%d" % (SLOTS + t)) for t in range(SLOTS)]
        for t in range(SLOTS):
            product(y_ps[t][:], w1, t, idx_w[:], idx_s[:])

        d_sum = sbuf("d_sum", [P, SLOTS, S], F32, "raw1_w")
        y_sum = sbuf("y_sum", [P, SLOTS, S], F32)
        d_sig = [sbuf("d_sig%d" % half, [P, SLOTS, S // 2], F32) for half in range(2)]
        for t in range(SLOTS):
            nc.scalar.copy(chain[t][:, :S], d_ps[t][:])
            nc.scalar.copy(chain[t + 1][:, S:], d_ps[t][:])
            nc.vector.tensor_tensor(d_sum[:, t, :], chain[t][:].indirect(n2_t[:]), chain[t + 1][:, S:], ALU.add)
        for t in range(SLOTS):
            u = SLOTS + t
            nc.scalar.activation(chain[u][:, :S], y_ps[t][:], ACT.Copy, scale=gain[:, t : t + 1])
            nc.scalar.activation(chain[u + 1][:, S:], y_ps[t][:], ACT.Copy, scale=gain[:, t : t + 1])
            nc.vector.tensor_tensor(y_sum[:, t, :], chain[u][:].indirect(n1_t[:]), chain[u + 1][:, S:], ALU.add)
        for half in range(2):
            nc.scalar.activation(d_sig[half][:], d_sum[:, :, HALVES[half]], ACT.Sigmoid)

        piece_sig = (d_sig[0][:], d_sig[1][:, :, : width(PIECES[1])], d_sig[1][:, :, width(PIECES[1]) :])
        z_bf = [sbuf("z_bf%d" % k, [P, width(cols) * SLOTS], BF16) for k, cols in enumerate(PIECES)]
        z_w = [sbuf("z_w%d" % k, [P, width(cols)], U32) for k, cols in enumerate(PIECES)]
        z_s = [sbuf("z_s%d" % k, [P, width(cols)], U8) for k, cols in enumerate(PIECES)]
        h_ps = [[None] * SLOTS for cols in PIECES]
        window = chain[:SLOTS]
        partner = [sbuf("partner%d" % t, [P, S], F32) for t in range(SLOTS)]
        neg_st = [sbuf("neg_st%d" % t, [P, S], F32) for t in range(SLOTS)]
        neg_st_plain = [sbuf("neg_st_plain%d" % t, [P, S], F32) for t in range(SLOTS)]

        def make_z(k):
            nc.vector.tensor_tensor(by_words(z_bf[k]), by_slots(y_sum[:, :, PIECES[k]]), by_slots(piece_sig[k]), ALU.mult)

        def make_h(k):
            nc.vector.quantize_mx(out=z_w[k][:].bitcast(FP8X4), scales=z_s[k][:], in_=z_bf[k][:])
            for t in range(SLOTS):
                h_ps[k][t] = psum.tile([P, width(PIECES[k])], F32, name="h_ps%d%d" % (k, t), tag="bank%d" % (SLOTS * (k % 2) + t))
                product(h_ps[k][t][:], w3, t, z_w[k][:], z_s[k][:])

        def leave_slot_0(k):
            nc.scalar.activation(window[0][:, PIECES[k]], h_ps[k][0][:], ACT.Sigmoid)
            nc.scalar.activation(partner[0][:, PIECES[k]], h_ps[k][0][:], ACT.Copy, scale=-1.0)

        def leave(copy, k, t):
            copy(window[t][:, PIECES[k]], h_ps[k][t][:])

        make_z(0)
        w3 = (deal_words("w3_w", raw3_w, "d_sig0"), w13_s, W3_ROW)
        make_h(0)
        leave_slot_0(0)
        leave(nc.scalar.copy, 0, 2)
        leave(nc.scalar.copy, 0, 3)
        make_z(1)
        make_z(2)
        make_h(1)
        leave(nc.vector.tensor_copy, 0, 1)
        make_h(2)
        leave_slot_0(1)
        leave_slot_0(2)
        for t in (1, 2):
            for k in (1, 2):
                leave(nc.vector.tensor_copy, k, t)

        result = [sbuf("result0", [P, SLOTS, width(PIECES[0])], F32)]

        def look_up_sigmoid(t):
            nc.scalar.activation(partner[t][:], window[t][:].indirect(n3_t[:]), ACT.Sigmoid)

        def make_neg_st(t):
            nc.vector.scalar_tensor_tensor(neg_st[t][:], window[t][:, :S], -1.0, partner[t][:], ALU.mult, ALU.mult)

        def make_result(k, t):
            cols = PIECES[k]
            nc.vector.tensor_tensor(result[k][:, t, :], neg_st[t][:].indirect(n4_t[:, cols.start // 16 : cols.stop // 16]), neg_st_plain[t][:, cols], ALU.subtract)

        nc.vector.tensor_tensor(neg_st[0][:], window[0][:].indirect(n3_t[:]), partner[0][:], ALU.mult)
        look_up_sigmoid(1)
        look_up_sigmoid(2)
        for k in (1, 2):
            leave(nc.scalar.copy, k, 3)
        look_up_sigmoid(3)
        make_neg_st(1)
        nc.vector.tensor_copy(neg_st_plain[0][:], neg_st[0][:])
        nc.vector.tensor_copy(neg_st_plain[1][:], neg_st[1][:])
        for t in (2, 3):
            make_result(0, t - 2)
            make_neg_st(t)
            nc.scalar.copy(neg_st_plain[t][:], neg_st[t][:])
        make_result(0, 2)
        make_result(0, 3)
        result.append(sbuf("result1", [P, SLOTS, width(PIECES[1])], F32, "partner3"))
        result.append(sbuf("result2", [P, SLOTS, width(PIECES[2])], F32, "chain3"))

        out_rows = out_0.rearrange("(p t) j -> p t j", t=SLOTS)
        out_bf = [sbuf("out_bf%d" % k, [P, width(cols) * SLOTS], BF16) for k, cols in enumerate(PIECES)]
        out_w = sbuf("out_w", [P, S], I32)
        out_s = sbuf("out_s", [P, S], U8)

        def store_and_round(k, copy):
            nc.sync.dma_start(out_rows[:, :, PIECES[k]], result[k][:])
            copy(by_words(out_bf[k]), by_slots(result[k][:]))

        def quantise_out(k):
            nc.vector.quantize_mx(out=out_w[:, PIECES[k]].bitcast(FP8X4), scales=out_s[:, PIECES[k]], in_=out_bf[k][:])

        def store_words(half):
            nc.sync.dma_start(words_of(out_1)[:, HALVES[half]], out_w[:, HALVES[half]])

        store_and_round(0, nc.scalar.copy)
        for t in range(SLOTS):
            make_result(1, t)
        store_and_round(1, nc.scalar.copy)
        make_result(2, 0)
        quantise_out(0)
        store_words(0)
        for t in range(1, SLOTS):
            make_result(2, t)
        store_and_round(2, nc.vector.tensor_copy)
        quantise_out(1)
        quantise_out(2)
        store_words(1)
        for q in range(QUADS):
            queue = nc.scalar if q % 2 else nc.sync
            queue.dma_start(out_2[0, 4 * q : 4 * q + 4, :].bitcast(I32), out_s[32 * q : 32 * q + 4, :].bitcast(I32))
